import numpy as np
import ml_dtypes


def mxq(x, axis, fmt="e4m3"):
    dtype, down = {"e4m3": (ml_dtypes.float8_e4m3fn, 7), "e5m2": (ml_dtypes.float8_e5m2, 14)}[fmt]
    v = np.moveaxis(np.asarray(x, np.float32).astype(ml_dtypes.bfloat16).astype(np.float64), axis, -1)
    blocks = v.reshape(v.shape[:-1] + (-1, 32))
    amax = np.abs(blocks).max(-1, keepdims=True)
    byte = np.maximum(np.where(amax > 0, np.frexp(amax)[1] - 1 + 127, 0) - down, 1)
    scale = np.exp2(byte - 127.0)
    codes = (blocks / scale).astype(np.float32).astype(dtype).astype(np.float64)
    return np.moveaxis((codes * scale).reshape(v.shape), -1, axis)


WIDE = False


def mx_kscale(k):
    if not WIDE:
        return np.ones(k)
    levels = np.array([10, -10, 5, -5, 0])
    if k % 512:
        return np.exp2(np.random.permutation(np.resize(levels, k // 32))).repeat(32)
    a = np.empty((k // 512, 16))
    for p in range(k // 512):
        a[p, :8] = np.random.permutation(np.resize(levels, 8))
        for g in range(8):
            far = levels[np.abs(levels - a[p, g]) >= 10]
            a[p, g + 8] = far[np.random.randint(len(far))]
    return np.exp2(a.ravel()).repeat(32)


def f64(x):
    return np.asarray(x).astype(np.float64)


def striped(idx):
    return np.tile(idx.reshape(-1, 16).T, (8, 1)).astype(np.uint16)


def unstriped(offs):
    return offs[:16].T.reshape(-1).astype(np.int64)


K, T, D, S, V, N = 1024, 512, 2, 512, 256, 512


def setup_inputs():
    n = np.random.standard_normal
    s = mx_kscale(K)[:, None]
    return {
        "xT": (n((K, T)) * s).astype(np.float32),
        "w": (n((D, K, N)) / np.sqrt(K) / s[None]).astype(np.float32),
        "offs": striped(np.random.permutation(T)[:S]),
    }


def reference(xT, w, offs):
    idx = unstriped(offs)
    xq = mxq(f64(xT)[:, idx], 0, "e4m3")
    wq = mxq(f64(w), 1, "e4m3")
    y0 = wq[0].T @ xq[:, :V]
    y1 = wq[1].T @ xq[:, V:]
    return y0 * y1

@@ -1,0 +1,168 @@
+from contextlib import ExitStack
+
+import concourse.mybir as mybir
+
+K, T, D, V, N = 1024, 512, 2, 256, 512
+FLOPS = 2 * D * K * N * V
+
+F32 = mybir.dt.float32
+BF16 = mybir.dt.bfloat16
+U32 = mybir.dt.uint32
+U16 = mybir.dt.uint16
+U8 = mybir.dt.uint8
+FP8X4 = mybir.dt.float8_e4m3fn_x4
+MULT = mybir.AluOpType.mult
+
+P = 128
+PACK = 4
+K_PASS = P * PACK
+PASSES = K // K_PASS
+M_TILES = N // P
+
+
+def tile_picked_pair_lin_mul_sub_e_kernel(tc, xT, w, offs, out):
+    nc = tc.nc
+    with ExitStack() as ctx:
+        keep = ctx.enter_context(tc.tile_pool(name="keep", bufs=1))
+        psum = ctx.enter_context(tc.psum_pool(name="psum", bufs=1))
+
+        offsets = keep.tile([P, D * V // 16], U16, name="offsets")
+        x_codes = [keep.tile([P, T], U32, name=f"x_codes{a}", align_bytes=64) for a in range(PASSES)]
+        x_scales = keep.tile([P, T], U8, name="x_scales", align_bytes=64)
+        nc.gpsimd.memset(x_scales[:], 0)
+        warm = keep.tile([P, 8], F32, name="warm")
+        warmed = keep.tile([P, 8], F32, name="warmed")
+        nc.vector.memset(warm[:], 0.0)
+        nc.scalar.copy(warmed[:], warm[:])
+
+        w_codes = [[keep.tile([P, N], U32, name=f"w_codes{d}{a}", align_bytes=64) for a in range(PASSES)] for d in range(D)]
+        w_scales = [[keep.tile([P, N], U8, name=f"w_scales{d}{a}", align_bytes=64) for a in range(PASSES)] for d in range(D)]
+
+        def load(name, rows, c0, c1):
+            raw = keep.tile([P, PACK, c1 - c0], F32, name=name)
+            nc.sync.dma_start(out=raw[:], in_=rows[:, c0:c1].rearrange("(p j) c -> p j c", j=PACK))
+            return raw
+
+        def interleave(engine, grouped, raw, c0, c1):
+            dst = grouped[:, c0:c1, :].rearrange("p (c i) t -> p c t i", i=4)
+            src = raw[:, :, c0:c1].rearrange("p t (c i) -> p c t i", i=4)
+            if engine == "v":
+                nc.vector.tensor_copy(dst, src)
+            else:
+                nc.scalar.copy(dst, src)
+
+        def quantize(grouped, codes, scales, g0, c0, n):
+            nc.vector.quantize_mx(
+                out=codes[:, c0 : c0 + n].bitcast(FP8X4),
+                scales=scales[:, c0 : c0 + n],
+                in_=grouped[:, g0 : g0 + n, :].rearrange("p c t -> p (c t)"),
+            )
+
+        def x_rows(a):
+            return xT[a * K_PASS : (a + 1) * K_PASS, :]
+
+        def w_rows(d, a):
+            return w[d, a * K_PASS : (a + 1) * K_PASS, :]
+
+        chunks = [
+            ("x", 0, 0, 0, 256, (("v", 128), ("s", 128))),
+            ("x", 0, 0, 256, 512, (("v", 128), ("s", 128))),
+            ("x", 0, 1, 0, 512, (("v", 128), ("s", 128), ("v", 128), ("s", 128))),
+            ("w", 0, 0, 0, 512, (("s", 128), ("s", 128), ("s", 128), ("v", 128))),
+            ("w", 0, 1, 0, 512, (("s", 128), ("s", 128), ("s", 128), ("v", 128))),
+            ("w", 1, 0, 0, 512, (("s", 128), ("s", 128), ("s", 128), ("v", 128))),
+            ("w", 1, 1, 0, 256, (("v", 128), ("s", 128))),
+            ("w", 1, 1, 256, 512, (("v", 128), ("s", 128))),
+        ]
+        raws = []
+        for i, (kind, d, a, c0, c1, splits) in enumerate(chunks):
+            rows = x_rows(a) if kind == "x" else w_rows(d, a)
+            raws.append(load(f"raw{i}", rows, c0, c1))
+            if i == 1:
+                nc.sync.dma_start(offsets[:], offs)
+
+        grouped = [keep.tile([P, c[4] - c[3], PACK], BF16, name=f"grouped{i}", align_bytes=64) for i, c in enumerate(chunks)]
+
+        def do_interleave(i):
+            g = 0
+            for engine, n in chunks[i][5]:
+                interleave(engine, grouped[i], raws[i], g, g + n)
+                g += n
+
+        def do_quantize(i, step):
+            kind, d, a, c0, c1, splits = chunks[i]
+            for g in range(0, c1 - c0, step):
+                if kind == "x":
+                    quantize(grouped[i], x_codes[a], x_scales[4 * a : P, :], g, c0 + g, step)
+                else:
+                    quantize(grouped[i], w_codes[d][a], w_scales[d][a], g, c0 + g, step)
+
+        p_codes = [[keep.tile([P, V], U32, name=f"p_codes{d}{a}", align_bytes=64) for a in range(PASSES)] for d in range(D)]
+        p_scales = [keep.tile([P, V], U8, name=f"p_scales{d}", align_bytes=64) for d in range(D)]
+
+        def entries(d):
+            return offsets[:, d * V // 16 : (d + 1) * V // 16]
+
+        def gather_words(d, a):
+            nc.vector.tensor_copy(p_codes[d][a][:], x_codes[a][:].indirect(entries(d)))
+
+        def gather_bytes(d):
+            nc.vector.tensor_copy(p_scales[d][:], x_scales[:].indirect(entries(d)))
+
+        y = [[psum.tile([P, V], F32, name=f"y{d}{m}") for m in range(M_TILES)] for d in range(D)]
+
+        def multiply(d, a, m):
+            cols = slice(m * P, (m + 1) * P)
+            nc.tensor.matmul_mx(
+                out=y[d][m][:],
+                lhsT=w_codes[d][a][:, cols].bitcast(FP8X4),
+                lhsT_scale=w_scales[d][a][:, cols],
+                rhs=p_codes[d][a][:].bitcast(FP8X4),
+                rhs_scale=p_scales[d][4 * a : P, :],
+                start=(a == 0),
+                stop=(a == PASSES - 1),
+            )
+
+        y0 = [keep.tile([P, V], F32, name=f"first{m}") for m in range(M_TILES)]
+        res = [keep.tile([P, V], F32, name=f"res{m}") for m in range(M_TILES)]
+
+        def finish(m):
+            nc.vector.tensor_tensor(res[m][:], y[1][m][:], y0[m][:], MULT)
+            nc.sync.dma_start(out=out[m * P : (m + 1) * P, :], in_=res[m][:])
+
+        do_interleave(0)
+        do_interleave(1)
+        do_quantize(0, 256)
+        do_interleave(2)
+        do_quantize(1, 256)
+        do_interleave(3)
+        do_quantize(2, 256)
+        gather_words(0, 0)
+        gather_bytes(0)
+        gather_words(0, 1)
+        do_quantize(3, 256)
+        for m in range(M_TILES):
+            multiply(0, 0, m)
+        do_interleave(4)
+        gather_words(1, 0)
+        gather_bytes(1)
+        do_quantize(4, 256)
+        for m in range(M_TILES):
+            multiply(0, 1, m)
+        do_interleave(5)
+        gather_words(1, 1)
+        do_quantize(5, 256)
+        for m in range(M_TILES):
+            nc.scalar.copy(y0[m][:], y[0][m][:])
+        for m in range(M_TILES):
+            multiply(1, 0, m)
+        do_interleave(6)
+        do_interleave(7)
+        do_quantize(6, 128)
+        for m in (0, 1):
+            multiply(1, 1, m)
+        do_quantize(7, 128)
+        for m in (2, 3):
+            multiply(1, 1, m)
+        for m in range(M_TILES):
+            finish(m)

@@ -7,6 +7,7 @@ FLOPS = 2 * D * K * N * V
 
 F32 = mybir.dt.float32
 BF16 = mybir.dt.bfloat16
+I32 = mybir.dt.int32
 U32 = mybir.dt.uint32
 U16 = mybir.dt.uint16
 U8 = mybir.dt.uint8
@@ -15,6 +16,7 @@ MULT = mybir.AluOpType.mult
 
 P = 128
 PACK = 4
+WINDOW = 704
 K_PASS = P * PACK
 PASSES = K // K_PASS
 M_TILES = N // P
@@ -27,9 +29,11 @@ def tile_picked_pair_lin_mul_sub_e_kernel(tc, xT, w, offs, out):
         psum = ctx.enter_context(tc.psum_pool(name="psum", bufs=1))
 
         offsets = keep.tile([P, D * V // 16], U16, name="offsets")
-        x_codes = [keep.tile([P, T], U32, name=f"x_codes{a}", align_bytes=64) for a in range(PASSES)]
-        x_scales = keep.tile([P, T], U8, name="x_scales", align_bytes=64)
+        x_codes = [keep.tile([P, WINDOW], I32, name=f"x_codes{a}", align_bytes=64) for a in range(PASSES)]
+        x_scales = keep.tile([P, WINDOW], U8, name="x_scales", align_bytes=64)
         nc.gpsimd.memset(x_scales[:], 0)
+        for a in range(PASSES):
+            nc.vector.memset(x_codes[a][:, T:WINDOW], 0)
         warm = keep.tile([P, 8], F32, name="warm")
         warmed = keep.tile([P, 8], F32, name="warmed")
         nc.vector.memset(warm[:], 0.0)
@@ -65,20 +69,19 @@ def tile_picked_pair_lin_mul_sub_e_kernel(tc, xT, w, offs, out):
             return w[d, a * K_PASS : (a + 1) * K_PASS, :]
 
         chunks = [
-            ("x", 0, 0, 0, 256, (("v", 128), ("s", 128))),
-            ("x", 0, 0, 256, 512, (("v", 128), ("s", 128))),
-            ("x", 0, 1, 0, 512, (("v", 128), ("s", 128), ("v", 128), ("s", 128))),
-            ("w", 0, 0, 0, 512, (("s", 128), ("s", 128), ("s", 128), ("v", 128))),
-            ("w", 0, 1, 0, 512, (("s", 128), ("s", 128), ("s", 128), ("v", 128))),
-            ("w", 1, 0, 0, 512, (("s", 128), ("s", 128), ("s", 128), ("v", 128))),
-            ("w", 1, 1, 0, 256, (("v", 128), ("s", 128))),
-            ("w", 1, 1, 256, 512, (("v", 128), ("s", 128))),
+            ("x", 0, 0, 0, 512, (("v", 368), ("s", 144))),
+            ("x", 0, 1, 0, 512, (("v", 128), ("s", 384))),
+            ("w", 0, 0, 0, 512, (("v", 64), ("s", 448))),
+            ("w", 0, 1, 0, 512, (("v", 48), ("s", 464))),
+            ("w", 1, 0, 0, 512, (("v", 176), ("s", 336))),
+            ("w", 1, 1, 0, 256, (("v", 144), ("s", 112))),
+            ("w", 1, 1, 256, 512, (("v", 176), ("s", 80))),
         ]
         raws = []
         for i, (kind, d, a, c0, c1, splits) in enumerate(chunks):
             rows = x_rows(a) if kind == "x" else w_rows(d, a)
             raws.append(load(f"raw{i}", rows, c0, c1))
-            if i == 1:
+            if i == 0:
                 nc.sync.dma_start(offsets[:], offs)
 
         grouped = [keep.tile([P, c[4] - c[3], PACK], BF16, name=f"grouped{i}", align_bytes=64) for i, c in enumerate(chunks)]
@@ -97,28 +100,26 @@ def tile_picked_pair_lin_mul_sub_e_kernel(tc, xT, w, offs, out):
                 else:
                     quantize(grouped[i], w_codes[d][a], w_scales[d][a], g, c0 + g, step)
 
-        p_codes = [[keep.tile([P, V], U32, name=f"p_codes{d}{a}", align_bytes=64) for a in range(PASSES)] for d in range(D)]
-        p_scales = [keep.tile([P, V], U8, name=f"p_scales{d}", align_bytes=64) for d in range(D)]
+        p_codes = [keep.tile([P, D * V], U32, name=f"p_codes{a}", align_bytes=64) for a in range(PASSES)]
+        p_scales = keep.tile([P, D * V], U8, name="p_scales", align_bytes=64)
 
-        def entries(d):
-            return offsets[:, d * V // 16 : (d + 1) * V // 16]
+        def gather_words(a):
+            nc.vector.tensor_copy(p_codes[a][:], x_codes[a][:].bitcast(U32).indirect(offsets[:]))
 
-        def gather_words(d, a):
-            nc.vector.tensor_copy(p_codes[d][a][:], x_codes[a][:].indirect(entries(d)))
-
-        def gather_bytes(d):
-            nc.vector.tensor_copy(p_scales[d][:], x_scales[:].indirect(entries(d)))
+        def gather_bytes():
+            nc.vector.tensor_copy(p_scales[:], x_scales[:].indirect(offsets[:]))
 
         y = [[psum.tile([P, V], F32, name=f"y{d}{m}") for m in range(M_TILES)] for d in range(D)]
 
         def multiply(d, a, m):
             cols = slice(m * P, (m + 1) * P)
+            picked = slice(d * V, (d + 1) * V)
             nc.tensor.matmul_mx(
                 out=y[d][m][:],
                 lhsT=w_codes[d][a][:, cols].bitcast(FP8X4),
                 lhsT_scale=w_scales[d][a][:, cols],
-                rhs=p_codes[d][a][:].bitcast(FP8X4),
-                rhs_scale=p_scales[d][4 * a : P, :],
+                rhs=p_codes[a][:, picked].bitcast(FP8X4),
+                rhs_scale=p_scales[4 * a : P, picked],
                 start=(a == 0),
                 stop=(a == PASSES - 1),
             )
@@ -131,38 +132,35 @@ def tile_picked_pair_lin_mul_sub_e_kernel(tc, xT, w, offs, out):
             nc.sync.dma_start(out=out[m * P : (m + 1) * P, :], in_=res[m][:])
 
         do_interleave(0)
+        do_quantize(0, 512)
+        gather_words(0)
         do_interleave(1)
-        do_quantize(0, 256)
-        do_interleave(2)
         do_quantize(1, 256)
-        do_interleave(3)
-        do_quantize(2, 256)
-        gather_words(0, 0)
-        gather_bytes(0)
-        gather_words(0, 1)
-        do_quantize(3, 256)
+        gather_words(1)
+        gather_bytes()
+        do_interleave(2)
+        do_quantize(2, 512)
         for m in range(M_TILES):
             multiply(0, 0, m)
-        do_interleave(4)
-        gather_words(1, 0)
-        gather_bytes(1)
-        do_quantize(4, 256)
+        do_interleave(3)
+        do_quantize(3, 512)
         for m in range(M_TILES):
             multiply(0, 1, m)
+        do_interleave(4)
         do_interleave(5)
-        gather_words(1, 1)
-        do_quantize(5, 256)
-        for m in range(M_TILES):
-            nc.scalar.copy(y0[m][:], y[0][m][:])
+        do_quantize(4, 512)
         for m in range(M_TILES):
             multiply(1, 0, m)
-        do_interleave(6)
-        do_interleave(7)
-        do_quantize(6, 128)
+        do_quantize(5, 256)
         for m in (0, 1):
             multiply(1, 1, m)
-        do_quantize(7, 128)
+        for m in (0, 1):
+            nc.scalar.copy(y0[m][:], y[0][m][:])
+        do_interleave(6)
+        do_quantize(6, 256)
         for m in (2, 3):
             multiply(1, 1, m)
+        for m in (2, 3):
+            nc.scalar.copy(y0[m][:], y[0][m][:])
         for m in range(M_TILES):
             finish(m)

@@ -69,13 +69,14 @@ def tile_picked_pair_lin_mul_sub_e_kernel(tc, xT, w, offs, out):
             return w[d, a * K_PASS : (a + 1) * K_PASS, :]
 
         chunks = [
-            ("x", 0, 0, 0, 512, (("v", 368), ("s", 144))),
-            ("x", 0, 1, 0, 512, (("v", 128), ("s", 384))),
+            ("x", 0, 0, 0, 512, (("v", 352), ("s", 160))),
+            ("x", 0, 1, 0, 512, (("v", 144), ("s", 368))),
             ("w", 0, 0, 0, 512, (("v", 64), ("s", 448))),
-            ("w", 0, 1, 0, 512, (("v", 48), ("s", 464))),
+            ("w", 0, 1, 0, 512, (("v", 64), ("s", 448))),
             ("w", 1, 0, 0, 512, (("v", 176), ("s", 336))),
-            ("w", 1, 1, 0, 256, (("v", 144), ("s", 112))),
-            ("w", 1, 1, 256, 512, (("v", 176), ("s", 80))),
+            ("w", 1, 1, 0, 256, (("v", 192), ("s", 64))),
+            ("w", 1, 1, 256, 384, (("v", 32), ("s", 96))),
+            ("w", 1, 1, 384, 512, (("v", 96), ("s", 32))),
         ]
         raws = []
         for i, (kind, d, a, c0, c1, splits) in enumerate(chunks):
@@ -135,10 +136,10 @@ def tile_picked_pair_lin_mul_sub_e_kernel(tc, xT, w, offs, out):
         do_quantize(0, 512)
         gather_words(0)
         do_interleave(1)
-        do_quantize(1, 256)
+        do_quantize(1, 512)
+        do_interleave(2)
         gather_words(1)
         gather_bytes()
-        do_interleave(2)
         do_quantize(2, 512)
         for m in range(M_TILES):
             multiply(0, 0, m)
@@ -148,18 +149,22 @@ def tile_picked_pair_lin_mul_sub_e_kernel(tc, xT, w, offs, out):
             multiply(0, 1, m)
         do_interleave(4)
         do_interleave(5)
-        do_quantize(4, 512)
-        for m in range(M_TILES):
+        do_quantize(4, 256)
+        for m in (0, 1):
             multiply(1, 0, m)
         do_quantize(5, 256)
         for m in (0, 1):
             multiply(1, 1, m)
+        for m in (2, 3):
+            multiply(1, 0, m)
         for m in (0, 1):
             nc.scalar.copy(y0[m][:], y[0][m][:])
         do_interleave(6)
-        do_quantize(6, 256)
-        for m in (2, 3):
-            multiply(1, 1, m)
+        do_interleave(7)
+        do_quantize(6, 128)
+        multiply(1, 1, 2)
+        do_quantize(7, 128)
+        multiply(1, 1, 3)
         for m in (2, 3):
             nc.scalar.copy(y0[m][:], y[0][m][:])
         for m in range(M_TILES):

from contextlib import ExitStack

import concourse.mybir as mybir

K, T, D, V, N = 1024, 512, 2, 256, 512
FLOPS = 2 * D * K * N * V

F32 = mybir.dt.float32
BF16 = mybir.dt.bfloat16
I32 = mybir.dt.int32
U32 = mybir.dt.uint32
U16 = mybir.dt.uint16
U8 = mybir.dt.uint8
FP8X4 = mybir.dt.float8_e4m3fn_x4
MULT = mybir.AluOpType.mult

P = 128
PACK = 4
WINDOW = 704
K_PASS = P * PACK
PASSES = K // K_PASS
M_TILES = N // P


def tile_picked_pair_lin_mul_sub_e_kernel(tc, xT, w, offs, out):
    nc = tc.nc
    with ExitStack() as ctx:
        keep = ctx.enter_context(tc.tile_pool(name="keep", bufs=1))
        psum = ctx.enter_context(tc.psum_pool(name="psum", bufs=1))

        offsets = keep.tile([P, D * V // 16], U16, name="offsets")
        x_codes = [keep.tile([P, WINDOW], I32, name=f"x_codes{a}", align_bytes=64) for a in range(PASSES)]
        x_scales = keep.tile([P, WINDOW], U8, name="x_scales", align_bytes=64)
        nc.gpsimd.memset(x_scales[:], 0)
        for a in range(PASSES):
            nc.vector.memset(x_codes[a][:, T:WINDOW], 0)
        warm = keep.tile([P, 8], F32, name="warm")
        warmed = keep.tile([P, 8], F32, name="warmed")
        nc.vector.memset(warm[:], 0.0)
        nc.scalar.copy(warmed[:], warm[:])

        w_codes = [[keep.tile([P, N], U32, name=f"w_codes{d}{a}", align_bytes=64) for a in range(PASSES)] for d in range(D)]
        w_scales = [[keep.tile([P, N], U8, name=f"w_scales{d}{a}", align_bytes=64) for a in range(PASSES)] for d in range(D)]

        def load(name, rows, c0, c1):
            raw = keep.tile([P, PACK, c1 - c0], F32, name=name)
            nc.sync.dma_start(out=raw[:], in_=rows[:, c0:c1].rearrange("(p j) c -> p j c", j=PACK))
            return raw

        def interleave(engine, grouped, raw, c0, c1):
            dst = grouped[:, c0:c1, :].rearrange("p (c i) t -> p c t i", i=4)
            src = raw[:, :, c0:c1].rearrange("p t (c i) -> p c t i", i=4)
            if engine == "v":
                nc.vector.tensor_copy(dst, src)
            else:
                nc.scalar.copy(dst, src)

        def quantize(grouped, codes, scales, g0, c0, n):
            nc.vector.quantize_mx(
                out=codes[:, c0 : c0 + n].bitcast(FP8X4),
                scales=scales[:, c0 : c0 + n],
                in_=grouped[:, g0 : g0 + n, :].rearrange("p c t -> p (c t)"),
            )

        def x_rows(a):
            return xT[a * K_PASS : (a + 1) * K_PASS, :]

        def w_rows(d, a):
            return w[d, a * K_PASS : (a + 1) * K_PASS, :]

        chunks = [
            ("x", 0, 0, 0, 512, (("v", 352), ("s", 160))),
            ("x", 0, 1, 0, 512, (("v", 144), ("s", 368))),
            ("w", 0, 0, 0, 512, (("v", 64), ("s", 448))),
            ("w", 0, 1, 0, 512, (("v", 64), ("s", 448))),
            ("w", 1, 0, 0, 512, (("v", 176), ("s", 336))),
            ("w", 1, 1, 0, 256, (("v", 192), ("s", 64))),
            ("w", 1, 1, 256, 384, (("v", 32), ("s", 96))),
            ("w", 1, 1, 384, 512, (("v", 96), ("s", 32))),
        ]
        raws = []
        for i, (kind, d, a, c0, c1, splits) in enumerate(chunks):
            rows = x_rows(a) if kind == "x" else w_rows(d, a)
            raws.append(load(f"raw{i}", rows, c0, c1))
            if i == 0:
                nc.sync.dma_start(offsets[:], offs)

        grouped = [keep.tile([P, c[4] - c[3], PACK], BF16, name=f"grouped{i}", align_bytes=64) for i, c in enumerate(chunks)]

        def do_interleave(i):
            g = 0
            for engine, n in chunks[i][5]:
                interleave(engine, grouped[i], raws[i], g, g + n)
                g += n

        def do_quantize(i, step):
            kind, d, a, c0, c1, splits = chunks[i]
            for g in range(0, c1 - c0, step):
                if kind == "x":
                    quantize(grouped[i], x_codes[a], x_scales[4 * a : P, :], g, c0 + g, step)
                else:
                    quantize(grouped[i], w_codes[d][a], w_scales[d][a], g, c0 + g, step)

        p_codes = [keep.tile([P, D * V], U32, name=f"p_codes{a}", align_bytes=64) for a in range(PASSES)]
        p_scales = keep.tile([P, D * V], U8, name="p_scales", align_bytes=64)

        def gather_words(a):
            nc.vector.tensor_copy(p_codes[a][:], x_codes[a][:].bitcast(U32).indirect(offsets[:]))

        def gather_bytes():
            nc.vector.tensor_copy(p_scales[:], x_scales[:].indirect(offsets[:]))

        y = [[psum.tile([P, V], F32, name=f"y{d}{m}") for m in range(M_TILES)] for d in range(D)]

        def multiply(d, a, m):
            cols = slice(m * P, (m + 1) * P)
            picked = slice(d * V, (d + 1) * V)
            nc.tensor.matmul_mx(
                out=y[d][m][:],
                lhsT=w_codes[d][a][:, cols].bitcast(FP8X4),
                lhsT_scale=w_scales[d][a][:, cols],
                rhs=p_codes[a][:, picked].bitcast(FP8X4),
                rhs_scale=p_scales[4 * a : P, picked],
                start=(a == 0),
                stop=(a == PASSES - 1),
            )

        y0 = [keep.tile([P, V], F32, name=f"first{m}") for m in range(M_TILES)]
        res = [keep.tile([P, V], F32, name=f"res{m}") for m in range(M_TILES)]

        def finish(m):
            nc.vector.tensor_tensor(res[m][:], y[1][m][:], y0[m][:], MULT)
            nc.sync.dma_start(out=out[m * P : (m + 1) * P, :], in_=res[m][:])

        do_interleave(0)
        do_quantize(0, 512)
        gather_words(0)
        do_interleave(1)
        do_quantize(1, 512)
        do_interleave(2)
        gather_words(1)
        gather_bytes()
        do_quantize(2, 512)
        for m in range(M_TILES):
            multiply(0, 0, m)
        do_interleave(3)
        do_quantize(3, 512)
        for m in range(M_TILES):
            multiply(0, 1, m)
        do_interleave(4)
        do_interleave(5)
        do_quantize(4, 256)
        for m in (0, 1):
            multiply(1, 0, m)
        do_quantize(5, 256)
        for m in (0, 1):
            multiply(1, 1, m)
        for m in (2, 3):
            multiply(1, 0, m)
        for m in (0, 1):
            nc.scalar.copy(y0[m][:], y[0][m][:])
        do_interleave(6)
        do_interleave(7)
        do_quantize(6, 128)
        multiply(1, 1, 2)
        do_quantize(7, 128)
        multiply(1, 1, 3)
        for m in (2, 3):
            nc.scalar.copy(y0[m][:], y[0][m][:])
        for m in range(M_TILES):
            finish(m)
